import numpy as np
import ml_dtypes


def mxq(x, axis, fmt="e4m3"):
    dtype, down = {"e4m3": (ml_dtypes.float8_e4m3fn, 7), "e5m2": (ml_dtypes.float8_e5m2, 14)}[fmt]
    v = np.moveaxis(np.asarray(x, np.float32).astype(ml_dtypes.bfloat16).astype(np.float64), axis, -1)
    blocks = v.reshape(v.shape[:-1] + (-1, 32))
    amax = np.abs(blocks).max(-1, keepdims=True)
    byte = np.maximum(np.where(amax > 0, np.frexp(amax)[1] - 1 + 127, 0) - down, 1)
    scale = np.exp2(byte - 127.0)
    codes = (blocks / scale).astype(np.float32).astype(dtype).astype(np.float64)
    return np.moveaxis((codes * scale).reshape(v.shape), -1, axis)


WIDE = False


def mx_kscale(k):
    if not WIDE:
        return np.ones(k)
    levels = np.array([10, -10, 5, -5, 0])
    if k % 512:
        return np.exp2(np.random.permutation(np.resize(levels, k // 32))).repeat(32)
    a = np.empty((k // 512, 16))
    for p in range(k // 512):
        a[p, :8] = np.random.permutation(np.resize(levels, 8))
        for g in range(8):
            far = levels[np.abs(levels - a[p, g]) >= 10]
            a[p, g + 8] = far[np.random.randint(len(far))]
    return np.exp2(a.ravel()).repeat(32)


def f64(x):
    return np.asarray(x).astype(np.float64)


def striped(idx):
    return np.tile(np.asarray(idx).reshape(-1, 16).T, (8, 1)).astype(np.uint16)


def unstriped(offs):
    return offs[:16].T.reshape(-1).astype(np.int64)


E2M1 = np.array([0.0, 0.5, 1.0, 1.5, 2.0, 3.0, 4.0, 6.0, -0.0, -0.5, -1.0, -1.5, -2.0, -3.0, -4.0, -6.0])


def pack_weight(w, fmt):
    k, n = w.shape
    w = f64(np.asarray(w, np.float32).astype(ml_dtypes.bfloat16)).reshape(k // 32, 32, n)
    amax = np.abs(w).max(1)
    if fmt == "e4m3":
        byte = np.frexp(amax)[1] - 1 + 127 - 7
    else:
        mant, ex = np.frexp(amax / 6.0)
        byte = np.where(mant > 0.5, ex, ex - 1) + 127
    byte = np.clip(np.where(amax > 0, byte, 1), 1, 254)
    scaled = (w * np.exp2(127.0 - byte)[:, None, :]).reshape(k, n).astype(np.float32)
    by_word = np.ascontiguousarray(scaled.reshape(k // 512, 128, 4, n).transpose(0, 1, 3, 2))
    if fmt == "e4m3":
        words = by_word.astype(ml_dtypes.float8_e4m3fn).view(np.uint8)
    else:
        c = by_word.astype(ml_dtypes.float4_e2m1fn).view(np.uint8) & 0xF
        words = (c[..., 0::2] | (c[..., 1::2] << 4)).reshape(k // 512, 128, 2 * n)
    return np.ascontiguousarray(words), np.ascontiguousarray(byte.astype(np.uint8).reshape(k // 512, 16, n))


def unpack_weight(words, scales, fmt):
    g, _, n = scales.shape
    words = np.ascontiguousarray(words).reshape(g, 128, n, -1)
    if fmt == "e4m3":
        vals = words.view(ml_dtypes.float8_e4m3fn).astype(np.float64)
    else:
        nib = np.empty((g, 128, n, 4), np.uint8)
        nib[..., 0::2] = words & 0xF
        nib[..., 1::2] = words >> 4
        vals = E2M1[nib]
    vals = vals * np.repeat(np.exp2(scales.astype(np.float64) - 127.0), 8, axis=1)[..., None]
    return vals.transpose(0, 1, 3, 2).reshape(g * 512, n)


D, T, I, Q, M = 512, 2048, 512, 128, 2048


def setup_inputs():
    n = np.random.standard_normal
    idx = np.random.permutation(T)[:I]
    idx2 = np.random.permutation(T)[:I]
    idx3 = np.random.permutation(T)[:I]
    idx4 = np.random.permutation(M)[:I]
    fd = mx_kscale(D)
    keysp = pack_weight(n((D, T)) / fd[:, None], "e4m3")
    return {
        "query": (n((D, Q)) * 1.0 / np.sqrt(D) * fd[:, None]).astype(np.float32),
        "keys_words": keysp[0],
        "keys_scales": keysp[1],
        "lam": (np.random.uniform(0.3, 0.9, (Q, 1))).astype(np.float32),
        "pull": (np.random.uniform(0.3, 0.9, (Q, 1))).astype(np.float32),
        "old": (np.random.uniform(0.0, 2.0, (Q, M))).astype(np.float32),
        "fade": (np.random.uniform(0.3, 0.9, (Q, 1))).astype(np.float32),
        "offs": striped(idx),
        "offs2": striped(idx2),
        "offs3": striped(idx3),
        "offs4": striped(idx4),
    }


def reference(query, keys_words, keys_scales, lam, pull, old, fade, offs, offs2, offs3, offs4):
    idx = unstriped(offs)
    idx2 = unstriped(offs2)
    idx3 = unstriped(offs3)
    idx4 = unstriped(offs4)
    keysu = unpack_weight(keys_words, keys_scales, "e4m3")
    queryq = mxq(f64(query), 0, "e4m3")
    a = queryq.T @ keysu
    rv = np.log(np.exp(a[:, idx2]) + np.exp(a[:, idx3]))
    s = a[:, idx] - rv * f64(lam)
    p = np.exp(s - np.max(s, axis=1, keepdims=True))
    r = p / np.sum(p, axis=1, keepdims=True)
    r1 = np.pad(r, ((0, 0), (1, 0)))[:, :I]
    w = r - r1 * f64(pull)
    ws = w * 256.0
    wf = np.zeros((Q, M))
    wf[:, idx4] = ws
    y = f64(old) * f64(fade) + wf
    return y

@@ -1,0 +1,184 @@
+from contextlib import ExitStack
+
+import concourse.mybir as mybir
+
+D, T, I, Q, M = 512, 2048, 512, 128, 2048
+FLOPS = 2 * D * Q * T
+
+F32 = mybir.dt.float32
+BF16 = mybir.dt.bfloat16
+I32 = mybir.dt.int32
+U32 = mybir.dt.uint32
+U16 = mybir.dt.uint16
+U8 = mybir.dt.uint8
+FP8X4 = mybir.dt.float8_e4m3fn_x4
+ALU = mybir.AluOpType
+ACT = mybir.ActivationFunctionType
+AX = mybir.AxisListType
+
+P = 128
+PACK = 4
+PLANE = 512
+KEY_CHUNK = 1024
+SCORE_PIECES = (512, 512, 512, 256, 128, 128)
+RIVAL_PIECES = (192, 192, 128)
+FIRST_SCATTER = 128
+STORE_PIECES = (256, 512, 512, 512, 256)
+
+
+def runs(widths):
+    start = 0
+    result = []
+    for width in widths:
+        result.append(slice(start, start + width))
+        start = start + width
+    return result
+
+
+def listed(offsets, slots):
+    return offsets[:, slots.start // 16 : slots.stop // 16]
+
+
+def tile_attend_tworivals_stepwise_counts_kernel(
+    tc, query, keys_words, keys_scales, lam, pull, old, fade, offs, offs2, offs3, offs4, out
+):
+    nc = tc.nc
+    with ExitStack() as ctx:
+        lists = ctx.enter_context(tc.tile_pool(name="lists", bufs=1))
+        keep = ctx.enter_context(tc.tile_pool(name="keep", bufs=1))
+        psum = ctx.enter_context(tc.psum_pool(name="psum", bufs=1))
+
+        planes = keep.tile([P, PLANE], U8, name="planes", align_bytes=64)
+        nc.vector.memset(planes[:].bitcast(I32), 0)
+
+        q_raw = keep.tile([P, PACK, Q], F32, name="q_raw")
+        nc.sync.dma_start(out=q_raw[:], in_=query.rearrange("(p j) q -> p j q", j=PACK))
+
+        scale_rows = keys_scales[0].bitcast(I32)
+        for quad in range(4):
+            nc.scalar.dma_start(
+                out=planes[32 * quad : 32 * quad + 16, :].bitcast(I32),
+                in_=scale_rows[4 * quad : 4 * quad + 4, :].rearrange("f (j c) -> j f c", j=4),
+            )
+
+        words = keys_words[0].rearrange("p t r -> p (t r)")
+        key_tiles = []
+        for c in range(T // KEY_CHUNK):
+            chunk = keep.tile([P, KEY_CHUNK], U32, name="keys%d" % c, align_bytes=64)
+            nc.sync.dma_start(
+                out=chunk[:].bitcast(I32),
+                in_=words[:, PACK * KEY_CHUNK * c : PACK * KEY_CHUNK * (c + 1)].bitcast(I32),
+            )
+            key_tiles.append(chunk)
+
+        first_rival = lists.tile([P, I // 16], U16, name="first_rival")
+        nc.sync.dma_start(first_rival[:], offs2)
+        second_rival = lists.tile([P, I // 16], U16, name="second_rival")
+        nc.sync.dma_start(second_rival[:], offs3)
+        own_token = lists.tile([P, I // 16], U16, name="own_token")
+        nc.sync.dma_start(own_token[:], offs)
+        lam_col = keep.tile([P, 1], F32, name="lam_col")
+        nc.sync.dma_start(out=lam_col[:], in_=lam)
+        pull_col = keep.tile([P, 1], F32, name="pull_col")
+        nc.sync.dma_start(out=pull_col[:], in_=pull)
+        places = lists.tile([P, I // 16], U16, name="places")
+        nc.sync.dma_start(places[:], offs4)
+        fade_col = keep.tile([P, 1], F32, name="fade_col")
+        nc.sync.dma_start(out=fade_col[:], in_=fade)
+        old_sb = keep.tile([P, M], F32, name="old_sb")
+        nc.sync.dma_start(out=old_sb[:], in_=old)
+
+        placed = keep.tile([P, M], F32, name="placed")
+        nc.vector.memset(placed[:], 0.0)
+        pulled = keep.tile([P, I + 1], F32, name="pulled")
+        nc.scalar.activation(pulled[:, 0:1], placed[:, 0:1], ACT.Copy)
+
+        q_grouped = keep.tile([P, Q, PACK], BF16, name="q_grouped", align_bytes=64)
+        nc.vector.tensor_copy(
+            out=q_grouped[:].rearrange("p (c i) j -> p c j i", i=4),
+            in_=q_raw[:].rearrange("p j (c i) -> p c j i", i=4),
+        )
+        q_codes = keep.tile([P, Q], U32, name="q_codes", align_bytes=64)
+        q_scales = keep.tile([P, Q], U8, name="q_scales", align_bytes=64)
+        nc.vector.quantize_mx(
+            out=q_codes[:].bitcast(FP8X4),
+            scales=q_scales[:],
+            in_=q_grouped[:].rearrange("p q j -> p (q j)"),
+        )
+
+        a = keep.tile([P, T], F32, name="a")
+        for n, tokens in enumerate(runs(SCORE_PIECES)):
+            width = tokens.stop - tokens.start
+            bank = psum.tile([P, width], F32, name="bank%d" % n)
+            chunk, in_chunk = divmod(tokens.start, KEY_CHUNK)
+            plane, in_plane = divmod(tokens.start, PLANE)
+            nc.tensor.matmul_mx(
+                out=bank[:],
+                lhsT=q_codes[:].bitcast(FP8X4),
+                lhsT_scale=q_scales[:],
+                rhs=key_tiles[chunk][:, in_chunk : in_chunk + width].bitcast(FP8X4),
+                rhs_scale=planes[4 * plane : P, in_plane : in_plane + width],
+                start=True,
+                stop=True,
+            )
+            if n % 2 == 0:
+                nc.scalar.copy(a[:, tokens], bank[:])
+            else:
+                nc.vector.tensor_copy(a[:, tokens], bank[:])
+
+        x = keep.tile([P, I], F32, name="x")
+        nc.vector.tensor_copy(x[:], a[:].indirect(first_rival[:]))
+        gap = keep.tile([P, I], F32, name="gap")
+        dist = keep.tile([P, I], F32, name="dist")
+        small = keep.tile([P, I], F32, name="small")
+        for slots in runs(RIVAL_PIECES):
+            nc.vector.tensor_tensor(
+                gap[:, slots], a[:].indirect(listed(second_rival, slots)), x[:, slots], ALU.subtract
+            )
+            nc.scalar.activation(dist[:, slots], gap[:, slots], ACT.Abs)
+            nc.scalar.activation(small[:, slots], dist[:, slots], ACT.Exp, scale=-1.0)
+        tail = keep.tile([P, I], F32, name="tail")
+        nc.scalar.activation(tail[:], small[:], ACT.Ln, bias=1.0)
+
+        z = keep.tile([P, I], F32, name="z")
+        nc.vector.tensor_copy(z[:], a[:].indirect(own_token[:]))
+        larger = keep.tile([P, I], F32, name="larger")
+        nc.vector.scalar_tensor_tensor(larger[:], gap[:], 0.0, x[:], ALU.max, ALU.add)
+        neg_pull = keep.tile([P, 1], F32, name="neg_pull")
+        nc.vector.tensor_scalar_mul(neg_pull[:], pull_col[:], -1.0)
+        partial = keep.tile([P, I], F32, name="partial")
+        nc.vector.scalar_tensor_tensor(partial[:], larger[:], lam_col[:], z[:], ALU.mult, ALU.subtract)
+
+        neg_s = keep.tile([P, I], F32, name="neg_s", tag="scores_then_faded")
+        nc.vector.scalar_tensor_tensor(neg_s[:], tail[:], lam_col[:], partial[:], ALU.mult, ALU.add)
+        neg_max = keep.tile([P, 1], F32, name="neg_max")
+        nc.vector.tensor_reduce(neg_max[:], neg_s[:], AX.X, ALU.min)
+
+        head = slice(0, FIRST_SCATTER)
+        rest = slice(FIRST_SCATTER, I)
+        p = keep.tile([P, I], F32, name="p")
+        sums = keep.tile([P, 2], F32, name="sums")
+        for n, slots in enumerate((head, rest)):
+            nc.scalar.activation(
+                p[:, slots], neg_s[:, slots], ACT.Exp, bias=neg_max[:], scale=-1.0, accum_out=sums[:, n : n + 1]
+            )
+        sums_scaled = keep.tile([P, 2], F32, name="sums_scaled")
+        total = keep.tile([P, 1], F32, name="total")
+        nc.scalar.activation(sums_scaled[:], sums[:], ACT.Copy, scale=1.0 / 256.0, accum_out=total[:])
+        nc.vector.tensor_scalar_mul(pulled[:, 1 : FIRST_SCATTER + 1], p[:, head], neg_pull[:])
+        nc.scalar.activation(pulled[:, FIRST_SCATTER + 1 : I], p[:, FIRST_SCATTER : I - 1], ACT.Copy, scale=neg_pull[:])
+
+        nc.vector.tensor_tensor(placed[:].indirect(listed(places, head)), p[:, head], pulled[:, head], ALU.add)
+        factor = keep.tile([P, 1], F32, name="factor")
+        nc.vector.reciprocal(factor[:], total[:])
+        nc.vector.tensor_tensor(placed[:].indirect(listed(places, rest)), p[:, rest], pulled[:, rest], ALU.add)
+
+        faded = keep.tile([P, M], F32, name="faded", tag="scores_then_faded")
+        result = keep.tile([P, M], F32, name="result")
+        for cols in runs(STORE_PIECES):
+            nc.scalar.activation(faded[:, cols], old_sb[:, cols], ACT.Copy, scale=fade_col[:])
+        for cols in runs(STORE_PIECES):
+            nc.vector.scalar_tensor_tensor(
+                result[:, cols], placed[:, cols], factor[:], faded[:, cols], ALU.mult, ALU.add
+            )
+            nc.sync.dma_start(out=out[:, cols], in_=result[:, cols])

@@ -19,11 +19,11 @@ AX = mybir.AxisListType
 P = 128
 PACK = 4
 PLANE = 512
-KEY_CHUNK = 1024
-SCORE_PIECES = (512, 512, 512, 256, 128, 128)
-RIVAL_PIECES = (192, 192, 128)
-FIRST_SCATTER = 128
-STORE_PIECES = (256, 512, 512, 512, 256)
+KEY_LOADS = (512, 512, 512, 512)
+SCORE_PIECES = (512, 512, 256, 256, 256, 128, 128)
+RIVAL_PIECES = (256, 192, 64)
+FIRST_SCATTER = 160
+STORE_PIECES = (128, 384, 512, 512, 384, 128)
 
 
 def runs(widths):
@@ -56,20 +56,21 @@ def tile_attend_tworivals_stepwise_counts_kernel(
 
         scale_rows = keys_scales[0].bitcast(I32)
         for quad in range(4):
-            nc.scalar.dma_start(
+            queue = nc.sync if quad < 2 else nc.scalar
+            queue.dma_start(
                 out=planes[32 * quad : 32 * quad + 16, :].bitcast(I32),
                 in_=scale_rows[4 * quad : 4 * quad + 4, :].rearrange("f (j c) -> j f c", j=4),
             )
 
         words = keys_words[0].rearrange("p t r -> p (t r)")
         key_tiles = []
-        for c in range(T // KEY_CHUNK):
-            chunk = keep.tile([P, KEY_CHUNK], U32, name="keys%d" % c, align_bytes=64)
+        for c, tokens in enumerate(runs(KEY_LOADS)):
+            chunk = keep.tile([P, tokens.stop - tokens.start], U32, name="keys%d" % c, align_bytes=64)
             nc.sync.dma_start(
                 out=chunk[:].bitcast(I32),
-                in_=words[:, PACK * KEY_CHUNK * c : PACK * KEY_CHUNK * (c + 1)].bitcast(I32),
+                in_=words[:, PACK * tokens.start : PACK * tokens.stop].bitcast(I32),
             )
-            key_tiles.append(chunk)
+            key_tiles.append((tokens, chunk))
 
         first_rival = lists.tile([P, I // 16], U16, name="first_rival")
         nc.sync.dma_start(first_rival[:], offs2)
@@ -93,30 +94,36 @@ def tile_attend_tworivals_stepwise_counts_kernel(
         pulled = keep.tile([P, I + 1], F32, name="pulled")
         nc.scalar.activation(pulled[:, 0:1], placed[:, 0:1], ACT.Copy)
 
-        q_grouped = keep.tile([P, Q, PACK], BF16, name="q_grouped", align_bytes=64)
-        nc.vector.tensor_copy(
-            out=q_grouped[:].rearrange("p (c i) j -> p c j i", i=4),
-            in_=q_raw[:].rearrange("p j (c i) -> p c j i", i=4),
-        )
         q_codes = keep.tile([P, Q], U32, name="q_codes", align_bytes=64)
         q_scales = keep.tile([P, Q], U8, name="q_scales", align_bytes=64)
-        nc.vector.quantize_mx(
-            out=q_codes[:].bitcast(FP8X4),
-            scales=q_scales[:],
-            in_=q_grouped[:].rearrange("p q j -> p (q j)"),
-        )
+        halves = runs((Q // 2, Q // 2))
+        grouped = []
+        for n, rows in enumerate(halves):
+            half = keep.tile([P, Q // 2, PACK], BF16, name="q_grouped%d" % n, align_bytes=64)
+            nc.vector.tensor_copy(
+                out=half[:].rearrange("p (c i) j -> p c j i", i=4),
+                in_=q_raw[:, :, rows].rearrange("p j (c i) -> p c j i", i=4),
+            )
+            grouped.append(half)
+        for rows, half in zip(halves, grouped):
+            nc.vector.quantize_mx(
+                out=q_codes[:, rows].bitcast(FP8X4),
+                scales=q_scales[:, rows],
+                in_=half[:].rearrange("p q j -> p (q j)"),
+            )
 
         a = keep.tile([P, T], F32, name="a")
         for n, tokens in enumerate(runs(SCORE_PIECES)):
             width = tokens.stop - tokens.start
             bank = psum.tile([P, width], F32, name="bank%d" % n)
-            chunk, in_chunk = divmod(tokens.start, KEY_CHUNK)
+            loaded, chunk = [pair for pair in key_tiles if pair[0].start <= tokens.start < pair[0].stop][0]
+            in_chunk = tokens.start - loaded.start
             plane, in_plane = divmod(tokens.start, PLANE)
             nc.tensor.matmul_mx(
                 out=bank[:],
                 lhsT=q_codes[:].bitcast(FP8X4),
                 lhsT_scale=q_scales[:],
-                rhs=key_tiles[chunk][:, in_chunk : in_chunk + width].bitcast(FP8X4),
+                rhs=chunk[:, in_chunk : in_chunk + width].bitcast(FP8X4),
                 rhs_scale=planes[4 * plane : P, in_plane : in_plane + width],
                 start=True,
                 stop=True,
@@ -129,30 +136,44 @@ def tile_attend_tworivals_stepwise_counts_kernel(
         x = keep.tile([P, I], F32, name="x")
         nc.vector.tensor_copy(x[:], a[:].indirect(first_rival[:]))
         gap = keep.tile([P, I], F32, name="gap")
-        dist = keep.tile([P, I], F32, name="dist")
-        small = keep.tile([P, I], F32, name="small")
+        slant = keep.tile([P, I], F32, name="slant", tag="slant_then_larger")
         for slots in runs(RIVAL_PIECES):
             nc.vector.tensor_tensor(
                 gap[:, slots], a[:].indirect(listed(second_rival, slots)), x[:, slots], ALU.subtract
             )
-            nc.scalar.activation(dist[:, slots], gap[:, slots], ACT.Abs)
-            nc.scalar.activation(small[:, slots], dist[:, slots], ACT.Exp, scale=-1.0)
-        tail = keep.tile([P, I], F32, name="tail")
-        nc.scalar.activation(tail[:], small[:], ACT.Ln, bias=1.0)
-
+            nc.scalar.activation(slant[:, slots], gap[:, slots], ACT.Tanh, scale=0.5)
         z = keep.tile([P, I], F32, name="z")
         nc.vector.tensor_copy(z[:], a[:].indirect(own_token[:]))
-        larger = keep.tile([P, I], F32, name="larger")
-        nc.vector.scalar_tensor_tensor(larger[:], gap[:], 0.0, x[:], ALU.max, ALU.add)
+        steep = keep.tile([P, I], F32, name="steep")
+        nc.vector.scalar_tensor_tensor(steep[:], slant[:], -1.0, slant[:], ALU.mult, ALU.max)
+        warm_ln = keep.tile([P, 1], F32, name="warm_ln")
+        nc.scalar.activation(warm_ln[:], gap[:, I - 1 : I], ACT.Ln, scale=0.0, bias=1.0)
+        log_share = keep.tile([P, I], F32, name="log_share")
+        nc.scalar.activation(log_share[:], steep[:], ACT.Ln, scale=0.5, bias=0.5)
+        warm_exp = keep.tile([P, 1], F32, name="warm_exp")
+        nc.scalar.activation(warm_exp[:], steep[:, 0:1], ACT.Exp)
+
+        larger = keep.tile([P, I], F32, name="larger", tag="slant_then_larger")
+        slot_halves = runs((I // 2, I // 2))
+        for slots in slot_halves:
+            nc.vector.scalar_tensor_tensor(larger[:, slots], gap[:, slots], 0.0, x[:, slots], ALU.max, ALU.add)
         neg_pull = keep.tile([P, 1], F32, name="neg_pull")
         nc.vector.tensor_scalar_mul(neg_pull[:], pull_col[:], -1.0)
+        neg_lam = keep.tile([P, 1], F32, name="neg_lam")
+        nc.vector.tensor_scalar_mul(neg_lam[:], lam_col[:], -1.0)
         partial = keep.tile([P, I], F32, name="partial")
-        nc.vector.scalar_tensor_tensor(partial[:], larger[:], lam_col[:], z[:], ALU.mult, ALU.subtract)
+        for slots in slot_halves:
+            nc.vector.scalar_tensor_tensor(
+                partial[:, slots], larger[:, slots], neg_lam[:], z[:, slots], ALU.mult, ALU.add
+            )
 
-        neg_s = keep.tile([P, I], F32, name="neg_s", tag="scores_then_faded")
-        nc.vector.scalar_tensor_tensor(neg_s[:], tail[:], lam_col[:], partial[:], ALU.mult, ALU.add)
+        s = keep.tile([P, I], F32, name="s", tag="scores_then_faded")
+        for slots in slot_halves:
+            nc.vector.scalar_tensor_tensor(
+                s[:, slots], log_share[:, slots], lam_col[:], partial[:, slots], ALU.mult, ALU.add
+            )
         neg_max = keep.tile([P, 1], F32, name="neg_max")
-        nc.vector.tensor_reduce(neg_max[:], neg_s[:], AX.X, ALU.min)
+        nc.vector.tensor_reduce(neg_max[:], s[:], AX.X, ALU.max, negate=True)
 
         head = slice(0, FIRST_SCATTER)
         rest = slice(FIRST_SCATTER, I)
@@ -160,7 +181,7 @@ def tile_attend_tworivals_stepwise_counts_kernel(
         sums = keep.tile([P, 2], F32, name="sums")
         for n, slots in enumerate((head, rest)):
             nc.scalar.activation(
-                p[:, slots], neg_s[:, slots], ACT.Exp, bias=neg_max[:], scale=-1.0, accum_out=sums[:, n : n + 1]
+                p[:, slots], s[:, slots], ACT.Exp, bias=neg_max[:], accum_out=sums[:, n : n + 1]
             )
         sums_scaled = keep.tile([P, 2], F32, name="sums_scaled")
         total = keep.tile([P, 1], F32, name="total")

@@ -18,8 +18,11 @@ AX = mybir.AxisListType
 
 P = 128
 PACK = 4
-PLANE = 512
-KEY_LOADS = (512, 512, 512, 512)
+QUADRANTS = 4
+PER_COLUMN = 16
+WEIGHT_SCALE = 256.0
+
+KEY_CHUNK = 512
 SCORE_PIECES = (512, 512, 256, 256, 256, 128, 128)
 RIVAL_PIECES = (256, 192, 64)
 FIRST_SCATTER = 160
@@ -28,15 +31,15 @@ STORE_PIECES = (128, 384, 512, 512, 384, 128)
 
 def runs(widths):
     start = 0
-    result = []
+    slices = []
     for width in widths:
-        result.append(slice(start, start + width))
+        slices.append(slice(start, start + width))
         start = start + width
-    return result
+    return slices
 
 
 def listed(offsets, slots):
-    return offsets[:, slots.start // 16 : slots.stop // 16]
+    return offsets[:, slots.start // PER_COLUMN : slots.stop // PER_COLUMN]
 
 
 def tile_attend_tworivals_stepwise_counts_kernel(
@@ -48,41 +51,41 @@ def tile_attend_tworivals_stepwise_counts_kernel(
         keep = ctx.enter_context(tc.tile_pool(name="keep", bufs=1))
         psum = ctx.enter_context(tc.psum_pool(name="psum", bufs=1))
 
-        planes = keep.tile([P, PLANE], U8, name="planes", align_bytes=64)
+        planes = keep.tile([P, KEY_CHUNK], U8, name="planes", align_bytes=64)
         nc.vector.memset(planes[:].bitcast(I32), 0)
 
         q_raw = keep.tile([P, PACK, Q], F32, name="q_raw")
         nc.sync.dma_start(out=q_raw[:], in_=query.rearrange("(p j) q -> p j q", j=PACK))
 
         scale_rows = keys_scales[0].bitcast(I32)
-        for quad in range(4):
-            queue = nc.sync if quad < 2 else nc.scalar
+        for quad in range(QUADRANTS):
+            queue = nc.sync if quad < QUADRANTS // 2 else nc.scalar
             queue.dma_start(
                 out=planes[32 * quad : 32 * quad + 16, :].bitcast(I32),
-                in_=scale_rows[4 * quad : 4 * quad + 4, :].rearrange("f (j c) -> j f c", j=4),
+                in_=scale_rows[4 * quad : 4 * quad + 4, :].rearrange("f (j c) -> j f c", j=T // KEY_CHUNK),
             )
 
         words = keys_words[0].rearrange("p t r -> p (t r)")
-        key_tiles = []
-        for c, tokens in enumerate(runs(KEY_LOADS)):
-            chunk = keep.tile([P, tokens.stop - tokens.start], U32, name="keys%d" % c, align_bytes=64)
+        key_chunks = []
+        for c in range(T // KEY_CHUNK):
+            chunk = keep.tile([P, KEY_CHUNK], U32, name="keys%d" % c, align_bytes=64)
             nc.sync.dma_start(
                 out=chunk[:].bitcast(I32),
-                in_=words[:, PACK * tokens.start : PACK * tokens.stop].bitcast(I32),
+                in_=words[:, PACK * KEY_CHUNK * c : PACK * KEY_CHUNK * (c + 1)].bitcast(I32),
             )
-            key_tiles.append((tokens, chunk))
+            key_chunks.append(chunk)
 
-        first_rival = lists.tile([P, I // 16], U16, name="first_rival")
+        first_rival = lists.tile([P, I // PER_COLUMN], U16, name="first_rival")
         nc.sync.dma_start(first_rival[:], offs2)
-        second_rival = lists.tile([P, I // 16], U16, name="second_rival")
+        second_rival = lists.tile([P, I // PER_COLUMN], U16, name="second_rival")
         nc.sync.dma_start(second_rival[:], offs3)
-        own_token = lists.tile([P, I // 16], U16, name="own_token")
+        own_token = lists.tile([P, I // PER_COLUMN], U16, name="own_token")
         nc.sync.dma_start(own_token[:], offs)
         lam_col = keep.tile([P, 1], F32, name="lam_col")
         nc.sync.dma_start(out=lam_col[:], in_=lam)
         pull_col = keep.tile([P, 1], F32, name="pull_col")
         nc.sync.dma_start(out=pull_col[:], in_=pull)
-        places = lists.tile([P, I // 16], U16, name="places")
+        places = lists.tile([P, I // PER_COLUMN], U16, name="places")
         nc.sync.dma_start(places[:], offs4)
         fade_col = keep.tile([P, 1], F32, name="fade_col")
         nc.sync.dma_start(out=fade_col[:], in_=fade)
@@ -91,21 +94,21 @@ def tile_attend_tworivals_stepwise_counts_kernel(
 
         placed = keep.tile([P, M], F32, name="placed")
         nc.vector.memset(placed[:], 0.0)
-        pulled = keep.tile([P, I + 1], F32, name="pulled")
+        pulled = keep.tile([P, I], F32, name="pulled")
         nc.scalar.activation(pulled[:, 0:1], placed[:, 0:1], ACT.Copy)
 
         q_codes = keep.tile([P, Q], U32, name="q_codes", align_bytes=64)
         q_scales = keep.tile([P, Q], U8, name="q_scales", align_bytes=64)
-        halves = runs((Q // 2, Q // 2))
+        row_halves = runs((Q // 2, Q // 2))
         grouped = []
-        for n, rows in enumerate(halves):
+        for n, rows in enumerate(row_halves):
             half = keep.tile([P, Q // 2, PACK], BF16, name="q_grouped%d" % n, align_bytes=64)
             nc.vector.tensor_copy(
                 out=half[:].rearrange("p (c i) j -> p c j i", i=4),
                 in_=q_raw[:, :, rows].rearrange("p j (c i) -> p c j i", i=4),
             )
             grouped.append(half)
-        for rows, half in zip(halves, grouped):
+        for rows, half in zip(row_halves, grouped):
             nc.vector.quantize_mx(
                 out=q_codes[:, rows].bitcast(FP8X4),
                 scales=q_scales[:, rows],
@@ -116,15 +119,13 @@ def tile_attend_tworivals_stepwise_counts_kernel(
         for n, tokens in enumerate(runs(SCORE_PIECES)):
             width = tokens.stop - tokens.start
             bank = psum.tile([P, width], F32, name="bank%d" % n)
-            loaded, chunk = [pair for pair in key_tiles if pair[0].start <= tokens.start < pair[0].stop][0]
-            in_chunk = tokens.start - loaded.start
-            plane, in_plane = divmod(tokens.start, PLANE)
+            c, first = divmod(tokens.start, KEY_CHUNK)
             nc.tensor.matmul_mx(
                 out=bank[:],
                 lhsT=q_codes[:].bitcast(FP8X4),
                 lhsT_scale=q_scales[:],
-                rhs=chunk[:, in_chunk : in_chunk + width].bitcast(FP8X4),
-                rhs_scale=planes[4 * plane : P, in_plane : in_plane + width],
+                rhs=key_chunks[c][:, first : first + width].bitcast(FP8X4),
+                rhs_scale=planes[4 * c : P, first : first + width],
                 start=True,
                 stop=True,
             )
@@ -133,8 +134,10 @@ def tile_attend_tworivals_stepwise_counts_kernel(
             else:
                 nc.vector.tensor_copy(a[:, tokens], bank[:])
 
+        slot_halves = runs((I // 2, I // 2))
         x = keep.tile([P, I], F32, name="x")
-        nc.vector.tensor_copy(x[:], a[:].indirect(first_rival[:]))
+        for slots in slot_halves:
+            nc.vector.tensor_copy(x[:, slots], a[:].indirect(listed(first_rival, slots)))
         gap = keep.tile([P, I], F32, name="gap")
         slant = keep.tile([P, I], F32, name="slant", tag="slant_then_larger")
         for slots in runs(RIVAL_PIECES):
@@ -146,6 +149,7 @@ def tile_attend_tworivals_stepwise_counts_kernel(
         nc.vector.tensor_copy(z[:], a[:].indirect(own_token[:]))
         steep = keep.tile([P, I], F32, name="steep")
         nc.vector.scalar_tensor_tensor(steep[:], slant[:], -1.0, slant[:], ALU.mult, ALU.max)
+
         warm_ln = keep.tile([P, 1], F32, name="warm_ln")
         nc.scalar.activation(warm_ln[:], gap[:, I - 1 : I], ACT.Ln, scale=0.0, bias=1.0)
         log_share = keep.tile([P, I], F32, name="log_share")
@@ -154,7 +158,6 @@ def tile_attend_tworivals_stepwise_counts_kernel(
         nc.scalar.activation(warm_exp[:], steep[:, 0:1], ACT.Exp)
 
         larger = keep.tile([P, I], F32, name="larger", tag="slant_then_larger")
-        slot_halves = runs((I // 2, I // 2))
         for slots in slot_halves:
             nc.vector.scalar_tensor_tensor(larger[:, slots], gap[:, slots], 0.0, x[:, slots], ALU.max, ALU.add)
         neg_pull = keep.tile([P, 1], F32, name="neg_pull")
@@ -166,7 +169,6 @@ def tile_attend_tworivals_stepwise_counts_kernel(
             nc.vector.scalar_tensor_tensor(
                 partial[:, slots], larger[:, slots], neg_lam[:], z[:, slots], ALU.mult, ALU.add
             )
-
         s = keep.tile([P, I], F32, name="s", tag="scores_then_faded")
         for slots in slot_halves:
             nc.vector.scalar_tensor_tensor(
@@ -180,12 +182,10 @@ def tile_attend_tworivals_stepwise_counts_kernel(
         p = keep.tile([P, I], F32, name="p")
         sums = keep.tile([P, 2], F32, name="sums")
         for n, slots in enumerate((head, rest)):
-            nc.scalar.activation(
-                p[:, slots], s[:, slots], ACT.Exp, bias=neg_max[:], accum_out=sums[:, n : n + 1]
-            )
+            nc.scalar.activation(p[:, slots], s[:, slots], ACT.Exp, bias=neg_max[:], accum_out=sums[:, n : n + 1])
         sums_scaled = keep.tile([P, 2], F32, name="sums_scaled")
         total = keep.tile([P, 1], F32, name="total")
-        nc.scalar.activation(sums_scaled[:], sums[:], ACT.Copy, scale=1.0 / 256.0, accum_out=total[:])
+        nc.scalar.activation(sums_scaled[:], sums[:], ACT.Copy, scale=1.0 / WEIGHT_SCALE, accum_out=total[:])
         nc.vector.tensor_scalar_mul(pulled[:, 1 : FIRST_SCATTER + 1], p[:, head], neg_pull[:])
         nc.scalar.activation(pulled[:, FIRST_SCATTER + 1 : I], p[:, FIRST_SCATTER : I - 1], ACT.Copy, scale=neg_pull[:])
 

from contextlib import ExitStack

import concourse.mybir as mybir

D, T, I, Q, M = 512, 2048, 512, 128, 2048
FLOPS = 2 * D * Q * T

F32 = mybir.dt.float32
BF16 = mybir.dt.bfloat16
I32 = mybir.dt.int32
U32 = mybir.dt.uint32
U16 = mybir.dt.uint16
U8 = mybir.dt.uint8
FP8X4 = mybir.dt.float8_e4m3fn_x4
ALU = mybir.AluOpType
ACT = mybir.ActivationFunctionType
AX = mybir.AxisListType

P = 128
PACK = 4
QUADRANTS = 4
PER_COLUMN = 16
WEIGHT_SCALE = 256.0

KEY_CHUNK = 512
SCORE_PIECES = (512, 512, 256, 256, 256, 128, 128)
RIVAL_PIECES = (256, 192, 64)
FIRST_SCATTER = 160
STORE_PIECES = (128, 384, 512, 512, 384, 128)


def runs(widths):
    start = 0
    slices = []
    for width in widths:
        slices.append(slice(start, start + width))
        start = start + width
    return slices


def listed(offsets, slots):
    return offsets[:, slots.start // PER_COLUMN : slots.stop // PER_COLUMN]


def tile_attend_tworivals_stepwise_counts_kernel(
    tc, query, keys_words, keys_scales, lam, pull, old, fade, offs, offs2, offs3, offs4, out
):
    nc = tc.nc
    with ExitStack() as ctx:
        lists = ctx.enter_context(tc.tile_pool(name="lists", bufs=1))
        keep = ctx.enter_context(tc.tile_pool(name="keep", bufs=1))
        psum = ctx.enter_context(tc.psum_pool(name="psum", bufs=1))

        planes = keep.tile([P, KEY_CHUNK], U8, name="planes", align_bytes=64)
        nc.vector.memset(planes[:].bitcast(I32), 0)

        q_raw = keep.tile([P, PACK, Q], F32, name="q_raw")
        nc.sync.dma_start(out=q_raw[:], in_=query.rearrange("(p j) q -> p j q", j=PACK))

        scale_rows = keys_scales[0].bitcast(I32)
        for quad in range(QUADRANTS):
            queue = nc.sync if quad < QUADRANTS // 2 else nc.scalar
            queue.dma_start(
                out=planes[32 * quad : 32 * quad + 16, :].bitcast(I32),
                in_=scale_rows[4 * quad : 4 * quad + 4, :].rearrange("f (j c) -> j f c", j=T // KEY_CHUNK),
            )

        words = keys_words[0].rearrange("p t r -> p (t r)")
        key_chunks = []
        for c in range(T // KEY_CHUNK):
            chunk = keep.tile([P, KEY_CHUNK], U32, name="keys%d" % c, align_bytes=64)
            nc.sync.dma_start(
                out=chunk[:].bitcast(I32),
                in_=words[:, PACK * KEY_CHUNK * c : PACK * KEY_CHUNK * (c + 1)].bitcast(I32),
            )
            key_chunks.append(chunk)

        first_rival = lists.tile([P, I // PER_COLUMN], U16, name="first_rival")
        nc.sync.dma_start(first_rival[:], offs2)
        second_rival = lists.tile([P, I // PER_COLUMN], U16, name="second_rival")
        nc.sync.dma_start(second_rival[:], offs3)
        own_token = lists.tile([P, I // PER_COLUMN], U16, name="own_token")
        nc.sync.dma_start(own_token[:], offs)
        lam_col = keep.tile([P, 1], F32, name="lam_col")
        nc.sync.dma_start(out=lam_col[:], in_=lam)
        pull_col = keep.tile([P, 1], F32, name="pull_col")
        nc.sync.dma_start(out=pull_col[:], in_=pull)
        places = lists.tile([P, I // PER_COLUMN], U16, name="places")
        nc.sync.dma_start(places[:], offs4)
        fade_col = keep.tile([P, 1], F32, name="fade_col")
        nc.sync.dma_start(out=fade_col[:], in_=fade)
        old_sb = keep.tile([P, M], F32, name="old_sb")
        nc.sync.dma_start(out=old_sb[:], in_=old)

        placed = keep.tile([P, M], F32, name="placed")
        nc.vector.memset(placed[:], 0.0)
        pulled = keep.tile([P, I], F32, name="pulled")
        nc.scalar.activation(pulled[:, 0:1], placed[:, 0:1], ACT.Copy)

        q_codes = keep.tile([P, Q], U32, name="q_codes", align_bytes=64)
        q_scales = keep.tile([P, Q], U8, name="q_scales", align_bytes=64)
        row_halves = runs((Q // 2, Q // 2))
        grouped = []
        for n, rows in enumerate(row_halves):
            half = keep.tile([P, Q // 2, PACK], BF16, name="q_grouped%d" % n, align_bytes=64)
            nc.vector.tensor_copy(
                out=half[:].rearrange("p (c i) j -> p c j i", i=4),
                in_=q_raw[:, :, rows].rearrange("p j (c i) -> p c j i", i=4),
            )
            grouped.append(half)
        for rows, half in zip(row_halves, grouped):
            nc.vector.quantize_mx(
                out=q_codes[:, rows].bitcast(FP8X4),
                scales=q_scales[:, rows],
                in_=half[:].rearrange("p q j -> p (q j)"),
            )

        a = keep.tile([P, T], F32, name="a")
        for n, tokens in enumerate(runs(SCORE_PIECES)):
            width = tokens.stop - tokens.start
            bank = psum.tile([P, width], F32, name="bank%d" % n)
            c, first = divmod(tokens.start, KEY_CHUNK)
            nc.tensor.matmul_mx(
                out=bank[:],
                lhsT=q_codes[:].bitcast(FP8X4),
                lhsT_scale=q_scales[:],
                rhs=key_chunks[c][:, first : first + width].bitcast(FP8X4),
                rhs_scale=planes[4 * c : P, first : first + width],
                start=True,
                stop=True,
            )
            if n % 2 == 0:
                nc.scalar.copy(a[:, tokens], bank[:])
            else:
                nc.vector.tensor_copy(a[:, tokens], bank[:])

        slot_halves = runs((I // 2, I // 2))
        x = keep.tile([P, I], F32, name="x")
        for slots in slot_halves:
            nc.vector.tensor_copy(x[:, slots], a[:].indirect(listed(first_rival, slots)))
        gap = keep.tile([P, I], F32, name="gap")
        slant = keep.tile([P, I], F32, name="slant", tag="slant_then_larger")
        for slots in runs(RIVAL_PIECES):
            nc.vector.tensor_tensor(
                gap[:, slots], a[:].indirect(listed(second_rival, slots)), x[:, slots], ALU.subtract
            )
            nc.scalar.activation(slant[:, slots], gap[:, slots], ACT.Tanh, scale=0.5)
        z = keep.tile([P, I], F32, name="z")
        nc.vector.tensor_copy(z[:], a[:].indirect(own_token[:]))
        steep = keep.tile([P, I], F32, name="steep")
        nc.vector.scalar_tensor_tensor(steep[:], slant[:], -1.0, slant[:], ALU.mult, ALU.max)

        warm_ln = keep.tile([P, 1], F32, name="warm_ln")
        nc.scalar.activation(warm_ln[:], gap[:, I - 1 : I], ACT.Ln, scale=0.0, bias=1.0)
        log_share = keep.tile([P, I], F32, name="log_share")
        nc.scalar.activation(log_share[:], steep[:], ACT.Ln, scale=0.5, bias=0.5)
        warm_exp = keep.tile([P, 1], F32, name="warm_exp")
        nc.scalar.activation(warm_exp[:], steep[:, 0:1], ACT.Exp)

        larger = keep.tile([P, I], F32, name="larger", tag="slant_then_larger")
        for slots in slot_halves:
            nc.vector.scalar_tensor_tensor(larger[:, slots], gap[:, slots], 0.0, x[:, slots], ALU.max, ALU.add)
        neg_pull = keep.tile([P, 1], F32, name="neg_pull")
        nc.vector.tensor_scalar_mul(neg_pull[:], pull_col[:], -1.0)
        neg_lam = keep.tile([P, 1], F32, name="neg_lam")
        nc.vector.tensor_scalar_mul(neg_lam[:], lam_col[:], -1.0)
        partial = keep.tile([P, I], F32, name="partial")
        for slots in slot_halves:
            nc.vector.scalar_tensor_tensor(
                partial[:, slots], larger[:, slots], neg_lam[:], z[:, slots], ALU.mult, ALU.add
            )
        s = keep.tile([P, I], F32, name="s", tag="scores_then_faded")
        for slots in slot_halves:
            nc.vector.scalar_tensor_tensor(
                s[:, slots], log_share[:, slots], lam_col[:], partial[:, slots], ALU.mult, ALU.add
            )
        neg_max = keep.tile([P, 1], F32, name="neg_max")
        nc.vector.tensor_reduce(neg_max[:], s[:], AX.X, ALU.max, negate=True)

        head = slice(0, FIRST_SCATTER)
        rest = slice(FIRST_SCATTER, I)
        p = keep.tile([P, I], F32, name="p")
        sums = keep.tile([P, 2], F32, name="sums")
        for n, slots in enumerate((head, rest)):
            nc.scalar.activation(p[:, slots], s[:, slots], ACT.Exp, bias=neg_max[:], accum_out=sums[:, n : n + 1])
        sums_scaled = keep.tile([P, 2], F32, name="sums_scaled")
        total = keep.tile([P, 1], F32, name="total")
        nc.scalar.activation(sums_scaled[:], sums[:], ACT.Copy, scale=1.0 / WEIGHT_SCALE, accum_out=total[:])
        nc.vector.tensor_scalar_mul(pulled[:, 1 : FIRST_SCATTER + 1], p[:, head], neg_pull[:])
        nc.scalar.activation(pulled[:, FIRST_SCATTER + 1 : I], p[:, FIRST_SCATTER : I - 1], ACT.Copy, scale=neg_pull[:])

        nc.vector.tensor_tensor(placed[:].indirect(listed(places, head)), p[:, head], pulled[:, head], ALU.add)
        factor = keep.tile([P, 1], F32, name="factor")
        nc.vector.reciprocal(factor[:], total[:])
        nc.vector.tensor_tensor(placed[:].indirect(listed(places, rest)), p[:, rest], pulled[:, rest], ALU.add)

        faded = keep.tile([P, M], F32, name="faded", tag="scores_then_faded")
        result = keep.tile([P, M], F32, name="result")
        for cols in runs(STORE_PIECES):
            nc.scalar.activation(faded[:, cols], old_sb[:, cols], ACT.Copy, scale=fade_col[:])
        for cols in runs(STORE_PIECES):
            nc.vector.scalar_tensor_tensor(
                result[:, cols], placed[:, cols], factor[:], faded[:, cols], ALU.mult, ALU.add
            )
            nc.sync.dma_start(out=out[:, cols], in_=result[:, cols])
